import numpy as np
import ml_dtypes


def mxq(x, axis, fmt="e4m3"):
    dtype, down = {"e4m3": (ml_dtypes.float8_e4m3fn, 7), "e5m2": (ml_dtypes.float8_e5m2, 14)}[fmt]
    v = np.moveaxis(np.asarray(x, np.float32).astype(ml_dtypes.bfloat16).astype(np.float64), axis, -1)
    blocks = v.reshape(v.shape[:-1] + (-1, 32))
    amax = np.abs(blocks).max(-1, keepdims=True)
    byte = np.maximum(np.where(amax > 0, np.frexp(amax)[1] - 1 + 127, 0) - down, 1)
    scale = np.exp2(byte - 127.0)
    codes = (blocks / scale).astype(np.float32).astype(dtype).astype(np.float64)
    return np.moveaxis((codes * scale).reshape(v.shape), -1, axis)


WIDE = False


def mx_kscale(k, group=512):
    if not WIDE:
        return np.ones(k)
    levels = np.array([18, -18])
    if group != 512:
        return np.exp2(np.random.permutation(np.resize(levels, k // group))).repeat(group)
    if k % 512:
        return np.exp2(np.random.permutation(np.resize(levels, k // 32))).repeat(32)
    a = np.empty((k // 512, 16))
    for p in range(k // 512):
        a[p, :8] = np.random.permutation(np.resize(levels, 8))
        for g in range(8):
            far = levels[np.abs(levels - a[p, g]) >= 10]
            a[p, g + 8] = far[np.random.randint(len(far))]
    return np.exp2(a.ravel()).repeat(32)


def f64(x):
    return np.asarray(x).astype(np.float64)


H, D, N = 4, 128, 1024


def setup_inputs():
    n = np.random.standard_normal
    s = mx_kscale(D, 0)[:, None]
    S = n((H, D, 128)) / np.sqrt(D)
    return {
        "q": n((H, D, N)).astype(np.float32),
        "qa": (np.random.uniform(0.5, 2.0, (D, 1)) * s).astype(np.float32),
        "S": (S / s).astype(np.float32),
        "og": n((H, N, 128)).astype(np.float32),
    }


def reference(q, qa, S, og):
    fq = (np.square(f64(q)) + 0.125) * f64(qa)
    y = mxq(fq, 1, "e4m3").transpose(0, 2, 1) @ mxq(f64(S), 1, "e4m3")
    y = y / (1.0 + np.exp(-f64(og)))
    return y

@@ -1,0 +1,148 @@
+from contextlib import ExitStack
+
+import concourse.mybir as mybir
+
+H, D, N, E = 4, 128, 1024, 128
+FLOPS = 2 * H * N * D * E
+
+F32 = mybir.dt.float32
+BF16 = mybir.dt.bfloat16
+U32 = mybir.dt.uint32
+U8 = mybir.dt.uint8
+FP8X4 = mybir.dt.float8_e4m3fn_x4
+ACT = mybir.ActivationFunctionType
+ALU = mybir.AluOpType
+
+P = 128
+PACK = 4
+ROWS = D // PACK
+R = N // P
+GROUPS = 2
+RG = R // GROUPS
+CHUNKS = 4
+CW = N // CHUNKS
+CM = CW // R
+HALVES = 2
+HM = P // HALVES
+
+
+def tile_rows_read_sq_gate_kernel(tc, q, qa, S, og, out):
+    nc = tc.nc
+    with ExitStack() as ctx:
+        pool = ctx.enter_context(tc.tile_pool(name="sb", bufs=1))
+        psum = ctx.enter_context(tc.psum_pool(name="ps", bufs=1))
+        ctx.enter_context(tc.manual_schedule())
+
+        q_rows = q.rearrange("h (p j) n -> (h p) j n", j=PACK)
+        s_rows = S.rearrange("h (p j) e -> (h p) j e", j=PACK)
+
+        weight = pool.tile([P, PACK], F32, name="weight")
+        nc.scalar.dma_start(out=weight[:], in_=qa.rearrange("d o -> (d o)").partition_broadcast(H))
+
+        og_rows = [og[h].rearrange("(m r) e -> m (r e)", r=R) for h in range(H)]
+        early = (R - 1) * E
+        og_early = pool.tile([P, E], F32, name="og_early", align_bytes=64)
+        nc.scalar.dma_start(out=og_early[:], in_=og_rows[H - 1][:, early:])
+        gate = {}
+        for h in range(H):
+            gate[h] = pool.tile([P, R * E], F32, name="gate%d" % h, align_bytes=64)
+        nc.scalar.activation(out=gate[H - 1][:, early:], in_=og_early[:], func=ACT.Sigmoid)
+
+        q_raw = []
+        for c in range(CHUNKS):
+            t = pool.tile([P, PACK, CW], F32, name="q_raw%d" % c, align_bytes=64)
+            nc.sync.dma_start(out=t[:], in_=q_rows[:, :, c * CW : (c + 1) * CW])
+            q_raw.append(t)
+        s_raw = pool.tile([P, PACK, E], F32, name="s_raw", align_bytes=64)
+        nc.sync.dma_start(out=s_raw[:], in_=s_rows)
+        og_raw = []
+        for h in range(H):
+            width = early if h == H - 1 else R * E
+            t = pool.tile([P, width], F32, name="og_raw%d" % h, align_bytes=64)
+            nc.sync.dma_start(out=t[:], in_=og_rows[h][:, :width])
+            og_raw.append(t)
+
+        mapped = {}
+        for half in range(HALVES):
+            for g in range(GROUPS):
+                mapped[half, g] = pool.tile([P, RG, HM, PACK], BF16, name="mapped%d_%d" % (half, g), align_bytes=64)
+        q_codes = [pool.tile([P, P], U32, name="q_codes%d" % r, align_bytes=64) for r in range(R)]
+        q_scales = [pool.tile([P, P], U8, name="q_scales%d" % r, align_bytes=64) for r in range(R)]
+        s_bf = pool.tile([P, E, PACK], BF16, name="s_bf", align_bytes=64)
+        s_codes = pool.tile([P, E], U32, name="s_codes", align_bytes=64)
+        s_scales = pool.tile([P, E], U8, name="s_scales", align_bytes=64)
+        weight_row = pool.tile([P, CM, PACK], F32, name="weight_row", align_bytes=64)
+        nc.vector.tensor_copy(out=weight_row[:], in_=weight[:].unsqueeze(1).to_broadcast([P, CM, PACK]))
+        weight_bc = weight_row[:].rearrange("p m j -> p (m j)").unsqueeze(1).to_broadcast([P, RG, CM * PACK])
+
+        def map_queries(c, g):
+            sq = pool.tile([P, RG, CM, PACK], F32, name="sq%d_%d" % (c, g), align_bytes=64)
+            src = q_raw[c][:].rearrange("p j (m g r) -> p g m j r", g=GROUPS, r=RG)[:, g]
+            nc.scalar.activation(out=sq[:].rearrange("p r m j -> p m j r"), in_=src, func=ACT.Square)
+            half, part = divmod(c, CHUNKS // HALVES)
+            nc.vector.scalar_tensor_tensor(
+                out=mapped[half, g][:, :, part * CM : (part + 1) * CM, :].rearrange("p r m j -> p r (m j)"),
+                in0=sq[:].rearrange("p r m j -> p r (m j)"), scalar=0.125, in1=weight_bc, op0=ALU.add, op1=ALU.mult)
+
+        def quantise(half, g):
+            cols = slice(half * HM, (half + 1) * HM)
+            for i in range(RG):
+                r = g * RG + i
+                nc.vector.quantize_mx(out=q_codes[r][:, cols].bitcast(FP8X4), scales=q_scales[r][:, cols],
+                                      in_=mapped[half, g][:, i].rearrange("p m j -> p (m j)"))
+
+        sums = {}
+        for h in range(H):
+            for g in range(GROUPS):
+                sums[h, g] = psum.tile([P, RG, E], F32, name="sums%d_%d" % (h, g))
+        res = [pool.tile([P, R * E], F32, name="res%d" % h, align_bytes=64) for h in range(H)]
+
+        def multiply(h, r):
+            rows = slice(ROWS * h, ROWS * (h + 1))
+            g, i = divmod(r, RG)
+            nc.tensor.matmul_mx(out=sums[h, g][:, i, :], lhsT=q_codes[r][rows, :].bitcast(FP8X4),
+                                lhsT_scale=q_scales[r][rows, :], rhs=s_codes[rows, :].bitcast(FP8X4),
+                                rhs_scale=s_scales[rows, :], start=True, stop=True)
+
+        def multiply_group(h, g):
+            for i in range(RG):
+                multiply(h, g * RG + i)
+
+        def apply_gate(h, g):
+            lo, hi = g * RG * E, (g + 1) * RG * E
+            loaded = min(hi, og_raw[h].shape[1])
+            nc.scalar.activation(out=gate[h][:, lo:loaded], in_=og_raw[h][:, lo:loaded], func=ACT.Sigmoid)
+            nc.vector.tensor_tensor(out=res[h][:, lo:hi], in0=sums[h, g][:].rearrange("p r e -> p (r e)"),
+                                    in1=gate[h][:, lo:hi], op=ALU.mult)
+            if g == GROUPS - 1:
+                nc.sync.dma_start(out=out[h].rearrange("(m r) e -> m (r e)", r=R), in_=res[h][:])
+
+        map_queries(0, 0)
+        map_queries(0, 1)
+        map_queries(1, 0)
+        map_queries(1, 1)
+        quantise(0, 0)
+        map_queries(2, 0)
+        quantise(0, 1)
+        map_queries(2, 1)
+        map_queries(3, 0)
+        nc.scalar.copy(out=s_bf[:], in_=s_raw[:].rearrange("p j e -> p e j"))
+        quantise(1, 0)
+        nc.vector.quantize_mx(out=s_codes[:].bitcast(FP8X4), scales=s_scales[:],
+                              in_=s_bf[:].rearrange("p e j -> p (e j)"))
+        multiply_group(0, 0)
+        multiply_group(1, 0)
+        map_queries(3, 1)
+        apply_gate(0, 0)
+        quantise(1, 1)
+        multiply_group(0, 1)
+        multiply_group(1, 1)
+        for h in range(2, H):
+            for g in range(GROUPS):
+                multiply_group(h, g)
+        apply_gate(1, 0)
+        apply_gate(0, 1)
+        apply_gate(1, 1)
+        for h in range(2, H):
+            for g in range(GROUPS):
+                apply_gate(h, g)

@@ -16,14 +16,13 @@ ALU = mybir.AluOpType
 P = 128
 PACK = 4
 ROWS = D // PACK
-R = N // P
-GROUPS = 2
-RG = R // GROUPS
-CHUNKS = 4
-CW = N // CHUNKS
-CM = CW // R
 HALVES = 2
-HM = P // HALVES
+HN = N // HALVES
+R = HN // P
+LOAD_W = 256
+PIECE_W = 128
+PM = PIECE_W // R
+PIECES = HN // PIECE_W
 
 
 def tile_rows_read_sq_gate_kernel(tc, q, qa, S, og, out):
@@ -35,114 +34,89 @@ def tile_rows_read_sq_gate_kernel(tc, q, qa, S, og, out):
 
         q_rows = q.rearrange("h (p j) n -> (h p) j n", j=PACK)
         s_rows = S.rearrange("h (p j) e -> (h p) j e", j=PACK)
+        blocks = [(half, h) for half in range(HALVES) for h in range(H)]
 
-        weight = pool.tile([P, PACK], F32, name="weight")
-        nc.scalar.dma_start(out=weight[:], in_=qa.rearrange("d o -> (d o)").partition_broadcast(H))
+        def block_rows(x, half, h):
+            return x[h, half * HN : (half + 1) * HN, :].rearrange("(m r) e -> m (r e)", r=R)
 
-        og_rows = [og[h].rearrange("(m r) e -> m (r e)", r=R) for h in range(H)]
+        gate = {b: pool.tile([P, R * E], F32, name="gate%d_%d" % b, align_bytes=64) for b in blocks}
+        last = blocks[-1]
         early = (R - 1) * E
         og_early = pool.tile([P, E], F32, name="og_early", align_bytes=64)
-        nc.scalar.dma_start(out=og_early[:], in_=og_rows[H - 1][:, early:])
-        gate = {}
-        for h in range(H):
-            gate[h] = pool.tile([P, R * E], F32, name="gate%d" % h, align_bytes=64)
-        nc.scalar.activation(out=gate[H - 1][:, early:], in_=og_early[:], func=ACT.Sigmoid)
+        nc.sync.dma_start(out=og_early[:], in_=block_rows(og, *last)[:, early:])
+        weight = pool.tile([P, PACK], F32, name="weight")
+        nc.scalar.dma_start(out=weight[:], in_=qa.rearrange("d o -> (d o)").partition_broadcast(H))
+        nc.scalar.activation(out=gate[last][:, early:], in_=og_early[:], func=ACT.Sigmoid)
 
         q_raw = []
-        for c in range(CHUNKS):
-            t = pool.tile([P, PACK, CW], F32, name="q_raw%d" % c, align_bytes=64)
-            nc.sync.dma_start(out=t[:], in_=q_rows[:, :, c * CW : (c + 1) * CW])
-            q_raw.append(t)
         s_raw = pool.tile([P, PACK, E], F32, name="s_raw", align_bytes=64)
-        nc.sync.dma_start(out=s_raw[:], in_=s_rows)
-        og_raw = []
-        for h in range(H):
-            width = early if h == H - 1 else R * E
-            t = pool.tile([P, width], F32, name="og_raw%d" % h, align_bytes=64)
-            nc.sync.dma_start(out=t[:], in_=og_rows[h][:, :width])
-            og_raw.append(t)
+        for c in range(N // LOAD_W):
+            t = pool.tile([P, PACK, LOAD_W], F32, name="q_raw%d" % c, align_bytes=64)
+            nc.sync.dma_start(out=t[:], in_=q_rows[:, :, c * LOAD_W : (c + 1) * LOAD_W])
+            q_raw.append(t)
+            if (c + 1) * LOAD_W == HN:
+                nc.sync.dma_start(out=s_raw[:], in_=s_rows)
+        og_raw = {}
+        for b in blocks:
+            width = early if b == last else R * E
+            og_raw[b] = pool.tile([P, width], F32, name="og_raw%d_%d" % b, align_bytes=64)
+            nc.sync.dma_start(out=og_raw[b][:], in_=block_rows(og, *b)[:, :width])
 
-        mapped = {}
-        for half in range(HALVES):
-            for g in range(GROUPS):
-                mapped[half, g] = pool.tile([P, RG, HM, PACK], BF16, name="mapped%d_%d" % (half, g), align_bytes=64)
-        q_codes = [pool.tile([P, P], U32, name="q_codes%d" % r, align_bytes=64) for r in range(R)]
-        q_scales = [pool.tile([P, P], U8, name="q_scales%d" % r, align_bytes=64) for r in range(R)]
+        mapped = [pool.tile([P, R, P, PACK], BF16, name="mapped%d" % half, align_bytes=64) for half in range(HALVES)]
+        q_codes = [pool.tile([P, R * P], U32, name="q_codes%d" % half, align_bytes=64) for half in range(HALVES)]
+        q_scales = [pool.tile([P, R * P], U8, name="q_scales%d" % half, align_bytes=64) for half in range(HALVES)]
         s_bf = pool.tile([P, E, PACK], BF16, name="s_bf", align_bytes=64)
         s_codes = pool.tile([P, E], U32, name="s_codes", align_bytes=64)
         s_scales = pool.tile([P, E], U8, name="s_scales", align_bytes=64)
-        weight_row = pool.tile([P, CM, PACK], F32, name="weight_row", align_bytes=64)
-        nc.vector.tensor_copy(out=weight_row[:], in_=weight[:].unsqueeze(1).to_broadcast([P, CM, PACK]))
-        weight_bc = weight_row[:].rearrange("p m j -> p (m j)").unsqueeze(1).to_broadcast([P, RG, CM * PACK])
+        weight_row = pool.tile([P, PM, PACK], F32, name="weight_row", align_bytes=64)
+        nc.vector.tensor_copy(out=weight_row[:], in_=weight[:].unsqueeze(1).to_broadcast([P, PM, PACK]))
+        weight_bc = weight_row[:].rearrange("p m j -> p (m j)").unsqueeze(1).to_broadcast([P, R, PM * PACK])
+        sums = {b: psum.tile([P, R, E], F32, name="sums%d_%d" % b) for b in blocks}
 
-        def map_queries(c, g):
-            sq = pool.tile([P, RG, CM, PACK], F32, name="sq%d_%d" % (c, g), align_bytes=64)
-            src = q_raw[c][:].rearrange("p j (m g r) -> p g m j r", g=GROUPS, r=RG)[:, g]
+        def map_queries(half, piece):
+            n0 = half * HN + piece * PIECE_W
+            c, col = divmod(n0, LOAD_W)
+            sq = pool.tile([P, R, PM, PACK], F32, name="sq%d_%d" % (half, piece), align_bytes=64)
+            src = q_raw[c][:, :, col : col + PIECE_W].rearrange("p j (m r) -> p m j r", r=R)
             nc.scalar.activation(out=sq[:].rearrange("p r m j -> p m j r"), in_=src, func=ACT.Square)
-            half, part = divmod(c, CHUNKS // HALVES)
             nc.vector.scalar_tensor_tensor(
-                out=mapped[half, g][:, :, part * CM : (part + 1) * CM, :].rearrange("p r m j -> p r (m j)"),
-                in0=sq[:].rearrange("p r m j -> p r (m j)"), scalar=0.125, in1=weight_bc, op0=ALU.add, op1=ALU.mult)
+                out=mapped[half][:, :, piece * PM : (piece + 1) * PM, :].rearrange("p r m j -> p r (m j)"),
+                in0=sq[:].rearrange("p r m j -> p r (m j)"), scalar=0.125, in1=weight_bc,
+                op0=ALU.add, op1=ALU.mult)
 
-        def quantise(half, g):
-            cols = slice(half * HM, (half + 1) * HM)
-            for i in range(RG):
-                r = g * RG + i
-                nc.vector.quantize_mx(out=q_codes[r][:, cols].bitcast(FP8X4), scales=q_scales[r][:, cols],
-                                      in_=mapped[half, g][:, i].rearrange("p m j -> p (m j)"))
+        def quantise_queries(half):
+            nc.vector.quantize_mx(out=q_codes[half][:].bitcast(FP8X4), scales=q_scales[half][:],
+                                  in_=mapped[half][:].rearrange("p r m j -> p (r m j)"))
 
-        sums = {}
-        for h in range(H):
-            for g in range(GROUPS):
-                sums[h, g] = psum.tile([P, RG, E], F32, name="sums%d_%d" % (h, g))
-        res = [pool.tile([P, R * E], F32, name="res%d" % h, align_bytes=64) for h in range(H)]
+        def multiply(half):
+            for r in range(R):
+                cols = slice(r * P, (r + 1) * P)
+                for h in range(H):
+                    rows = slice(ROWS * h, ROWS * (h + 1))
+                    nc.tensor.matmul_mx(
+                        out=sums[half, h][:, r, :], lhsT=q_codes[half][rows, cols].bitcast(FP8X4),
+                        lhsT_scale=q_scales[half][rows, cols], rhs=s_codes[rows, :].bitcast(FP8X4),
+                        rhs_scale=s_scales[rows, :], start=True, stop=True)
 
-        def multiply(h, r):
-            rows = slice(ROWS * h, ROWS * (h + 1))
-            g, i = divmod(r, RG)
-            nc.tensor.matmul_mx(out=sums[h, g][:, i, :], lhsT=q_codes[r][rows, :].bitcast(FP8X4),
-                                lhsT_scale=q_scales[r][rows, :], rhs=s_codes[rows, :].bitcast(FP8X4),
-                                rhs_scale=s_scales[rows, :], start=True, stop=True)
+        def apply_gate(b):
+            width = og_raw[b].shape[1]
+            nc.scalar.activation(out=gate[b][:, :width], in_=og_raw[b][:], func=ACT.Sigmoid)
+            res = pool.tile([P, R * E], F32, name="res%d_%d" % b, align_bytes=64)
+            nc.vector.tensor_tensor(out=res[:], in0=sums[b][:].rearrange("p r e -> p (r e)"), in1=gate[b][:],
+                                    op=ALU.mult)
+            nc.sync.dma_start(out=block_rows(out, *b), in_=res[:])
 
-        def multiply_group(h, g):
-            for i in range(RG):
-                multiply(h, g * RG + i)
-
-        def apply_gate(h, g):
-            lo, hi = g * RG * E, (g + 1) * RG * E
-            loaded = min(hi, og_raw[h].shape[1])
-            nc.scalar.activation(out=gate[h][:, lo:loaded], in_=og_raw[h][:, lo:loaded], func=ACT.Sigmoid)
-            nc.vector.tensor_tensor(out=res[h][:, lo:hi], in0=sums[h, g][:].rearrange("p r e -> p (r e)"),
-                                    in1=gate[h][:, lo:hi], op=ALU.mult)
-            if g == GROUPS - 1:
-                nc.sync.dma_start(out=out[h].rearrange("(m r) e -> m (r e)", r=R), in_=res[h][:])
-
-        map_queries(0, 0)
-        map_queries(0, 1)
-        map_queries(1, 0)
-        map_queries(1, 1)
-        quantise(0, 0)
-        map_queries(2, 0)
-        quantise(0, 1)
-        map_queries(2, 1)
-        map_queries(3, 0)
+        for piece in range(PIECES):
+            map_queries(0, piece)
         nc.scalar.copy(out=s_bf[:], in_=s_raw[:].rearrange("p j e -> p e j"))
-        quantise(1, 0)
+        quantise_queries(0)
         nc.vector.quantize_mx(out=s_codes[:].bitcast(FP8X4), scales=s_scales[:],
                               in_=s_bf[:].rearrange("p e j -> p (e j)"))
-        multiply_group(0, 0)
-        multiply_group(1, 0)
-        map_queries(3, 1)
-        apply_gate(0, 0)
-        quantise(1, 1)
-        multiply_group(0, 1)
-        multiply_group(1, 1)
-        for h in range(2, H):
-            for g in range(GROUPS):
-                multiply_group(h, g)
-        apply_gate(1, 0)
-        apply_gate(0, 1)
-        apply_gate(1, 1)
-        for h in range(2, H):
-            for g in range(GROUPS):
-                apply_gate(h, g)
+        multiply(0)
+        for piece in range(PIECES):
+            map_queries(1, piece)
+        apply_gate(blocks[0])
+        quantise_queries(1)
+        multiply(1)
+        for b in blocks[1:]:
+            apply_gate(b)

@@ -23,6 +23,7 @@ LOAD_W = 256
 PIECE_W = 128
 PM = PIECE_W // R
 PIECES = HN // PIECE_W
+EARLY_W = 32
 
 
 def tile_rows_read_sq_gate_kernel(tc, q, qa, S, og, out):
@@ -41,11 +42,11 @@ def tile_rows_read_sq_gate_kernel(tc, q, qa, S, og, out):
 
         gate = {b: pool.tile([P, R * E], F32, name="gate%d_%d" % b, align_bytes=64) for b in blocks}
         last = blocks[-1]
-        early = (R - 1) * E
-        og_early = pool.tile([P, E], F32, name="og_early", align_bytes=64)
+        early = R * E - EARLY_W
+        og_early = pool.tile([P, EARLY_W], F32, name="og_early", align_bytes=64)
         nc.sync.dma_start(out=og_early[:], in_=block_rows(og, *last)[:, early:])
-        weight = pool.tile([P, PACK], F32, name="weight")
-        nc.scalar.dma_start(out=weight[:], in_=qa.rearrange("d o -> (d o)").partition_broadcast(H))
+        qa_row = pool.tile([P, D], F32, name="qa_row", align_bytes=64)
+        nc.scalar.dma_start(out=qa_row[0:P:ROWS, :], in_=qa.rearrange("d o -> (d o)").partition_broadcast(H))
         nc.scalar.activation(out=gate[last][:, early:], in_=og_early[:], func=ACT.Sigmoid)
 
         q_raw = []
@@ -62,14 +63,22 @@ def tile_rows_read_sq_gate_kernel(tc, q, qa, S, og, out):
             og_raw[b] = pool.tile([P, width], F32, name="og_raw%d_%d" % b, align_bytes=64)
             nc.sync.dma_start(out=og_raw[b][:], in_=block_rows(og, *b)[:, :width])
 
-        mapped = [pool.tile([P, R, P, PACK], BF16, name="mapped%d" % half, align_bytes=64) for half in range(HALVES)]
+        mapped = [pool.tile([P, R, P, PACK], BF16, name="mapped%d" % half, tag="mapped%d" % half, align_bytes=64)
+                  for half in range(HALVES)]
         q_codes = [pool.tile([P, R * P], U32, name="q_codes%d" % half, align_bytes=64) for half in range(HALVES)]
         q_scales = [pool.tile([P, R * P], U8, name="q_scales%d" % half, align_bytes=64) for half in range(HALVES)]
         s_bf = pool.tile([P, E, PACK], BF16, name="s_bf", align_bytes=64)
         s_codes = pool.tile([P, E], U32, name="s_codes", align_bytes=64)
         s_scales = pool.tile([P, E], U8, name="s_scales", align_bytes=64)
         weight_row = pool.tile([P, PM, PACK], F32, name="weight_row", align_bytes=64)
-        nc.vector.tensor_copy(out=weight_row[:], in_=weight[:].unsqueeze(1).to_broadcast([P, PM, PACK]))
+        qa_blocks = pool.tile([P, PACK, ROWS], F32, name="qa_blocks", align_bytes=64)
+        qa_turned = pool.tile([P, PACK, ROWS], F32, name="qa_turned", align_bytes=64)
+        nc.vector.memset(qa_blocks[:], 0.0)
+        for h in range(H):
+            first = slice(ROWS * h, ROWS * h + 1)
+            nc.vector.tensor_copy(out=qa_blocks[first], in_=qa_row[first, :].rearrange("o (p j) -> o j p", j=PACK))
+        nc.vector.transpose(out=qa_turned[:].rearrange("p j c -> p (j c)"), in_=qa_blocks[:].rearrange("p j c -> p (j c)"))
+        nc.vector.tensor_copy(out=weight_row[:], in_=qa_turned[:, :, 0].unsqueeze(1).to_broadcast([P, PM, PACK]))
         weight_bc = weight_row[:].rearrange("p m j -> p (m j)").unsqueeze(1).to_broadcast([P, R, PM * PACK])
         sums = {b: psum.tile([P, R, E], F32, name="sums%d_%d" % b) for b in blocks}
 
@@ -88,35 +97,38 @@ def tile_rows_read_sq_gate_kernel(tc, q, qa, S, og, out):
             nc.vector.quantize_mx(out=q_codes[half][:].bitcast(FP8X4), scales=q_scales[half][:],
                                   in_=mapped[half][:].rearrange("p r m j -> p (r m j)"))
 
-        def multiply(half):
+        def multiply(half, heads):
             for r in range(R):
                 cols = slice(r * P, (r + 1) * P)
-                for h in range(H):
+                for h in heads:
                     rows = slice(ROWS * h, ROWS * (h + 1))
                     nc.tensor.matmul_mx(
                         out=sums[half, h][:, r, :], lhsT=q_codes[half][rows, cols].bitcast(FP8X4),
                         lhsT_scale=q_scales[half][rows, cols], rhs=s_codes[rows, :].bitcast(FP8X4),
                         rhs_scale=s_scales[rows, :], start=True, stop=True)
 
-        def apply_gate(b):
-            width = og_raw[b].shape[1]
-            nc.scalar.activation(out=gate[b][:, :width], in_=og_raw[b][:], func=ACT.Sigmoid)
-            res = pool.tile([P, R * E], F32, name="res%d_%d" % b, align_bytes=64)
-            nc.vector.tensor_tensor(out=res[:], in0=sums[b][:].rearrange("p r e -> p (r e)"), in1=gate[b][:],
-                                    op=ALU.mult)
-            nc.sync.dma_start(out=block_rows(out, *b), in_=res[:])
+        def apply_gate(b, parts):
+            part_w = R * E // parts
+            for lo in range(0, R * E, part_w):
+                cols = slice(lo, lo + part_w)
+                fresh = slice(lo, min(lo + part_w, og_raw[b].shape[1]))
+                nc.scalar.activation(out=gate[b][:, fresh], in_=og_raw[b][:, fresh], func=ACT.Sigmoid)
+                res = pool.tile([P, part_w], F32, name="res%d_%d_%d" % (*b, lo), align_bytes=64)
+                nc.vector.tensor_tensor(out=res[:], in0=sums[b][:].rearrange("p r e -> p (r e)")[:, cols],
+                                        in1=gate[b][:, cols], op=ALU.mult)
+                nc.sync.dma_start(out=block_rows(out, *b)[:, cols], in_=res[:])
 
         for piece in range(PIECES):
             map_queries(0, piece)
         nc.scalar.copy(out=s_bf[:], in_=s_raw[:].rearrange("p j e -> p e j"))
-        quantise_queries(0)
         nc.vector.quantize_mx(out=s_codes[:].bitcast(FP8X4), scales=s_scales[:],
                               in_=s_bf[:].rearrange("p e j -> p (e j)"))
-        multiply(0)
+        quantise_queries(0)
+        multiply(0, range(H))
         for piece in range(PIECES):
             map_queries(1, piece)
-        apply_gate(blocks[0])
+        apply_gate((0, 0), 1)
         quantise_queries(1)
-        multiply(1)
+        multiply(1, range(H))
         for b in blocks[1:]:
-            apply_gate(b)
+            apply_gate(b, 1)

from contextlib import ExitStack

import concourse.mybir as mybir

H, D, N, E = 4, 128, 1024, 128
FLOPS = 2 * H * N * D * E

F32 = mybir.dt.float32
BF16 = mybir.dt.bfloat16
U32 = mybir.dt.uint32
U8 = mybir.dt.uint8
FP8X4 = mybir.dt.float8_e4m3fn_x4
ACT = mybir.ActivationFunctionType
ALU = mybir.AluOpType

P = 128
PACK = 4
ROWS = D // PACK
HALVES = 2
HN = N // HALVES
R = HN // P
LOAD_W = 256
PIECE_W = 128
PM = PIECE_W // R
PIECES = HN // PIECE_W
EARLY_W = 32


def tile_rows_read_sq_gate_kernel(tc, q, qa, S, og, out):
    nc = tc.nc
    with ExitStack() as ctx:
        pool = ctx.enter_context(tc.tile_pool(name="sb", bufs=1))
        psum = ctx.enter_context(tc.psum_pool(name="ps", bufs=1))
        ctx.enter_context(tc.manual_schedule())

        q_rows = q.rearrange("h (p j) n -> (h p) j n", j=PACK)
        s_rows = S.rearrange("h (p j) e -> (h p) j e", j=PACK)
        blocks = [(half, h) for half in range(HALVES) for h in range(H)]

        def block_rows(x, half, h):
            return x[h, half * HN : (half + 1) * HN, :].rearrange("(m r) e -> m (r e)", r=R)

        gate = {b: pool.tile([P, R * E], F32, name="gate%d_%d" % b, align_bytes=64) for b in blocks}
        last = blocks[-1]
        early = R * E - EARLY_W
        og_early = pool.tile([P, EARLY_W], F32, name="og_early", align_bytes=64)
        nc.sync.dma_start(out=og_early[:], in_=block_rows(og, *last)[:, early:])
        qa_row = pool.tile([P, D], F32, name="qa_row", align_bytes=64)
        nc.scalar.dma_start(out=qa_row[0:P:ROWS, :], in_=qa.rearrange("d o -> (d o)").partition_broadcast(H))
        nc.scalar.activation(out=gate[last][:, early:], in_=og_early[:], func=ACT.Sigmoid)

        q_raw = []
        s_raw = pool.tile([P, PACK, E], F32, name="s_raw", align_bytes=64)
        for c in range(N // LOAD_W):
            t = pool.tile([P, PACK, LOAD_W], F32, name="q_raw%d" % c, align_bytes=64)
            nc.sync.dma_start(out=t[:], in_=q_rows[:, :, c * LOAD_W : (c + 1) * LOAD_W])
            q_raw.append(t)
            if (c + 1) * LOAD_W == HN:
                nc.sync.dma_start(out=s_raw[:], in_=s_rows)
        og_raw = {}
        for b in blocks:
            width = early if b == last else R * E
            og_raw[b] = pool.tile([P, width], F32, name="og_raw%d_%d" % b, align_bytes=64)
            nc.sync.dma_start(out=og_raw[b][:], in_=block_rows(og, *b)[:, :width])

        mapped = [pool.tile([P, R, P, PACK], BF16, name="mapped%d" % half, tag="mapped%d" % half, align_bytes=64)
                  for half in range(HALVES)]
        q_codes = [pool.tile([P, R * P], U32, name="q_codes%d" % half, align_bytes=64) for half in range(HALVES)]
        q_scales = [pool.tile([P, R * P], U8, name="q_scales%d" % half, align_bytes=64) for half in range(HALVES)]
        s_bf = pool.tile([P, E, PACK], BF16, name="s_bf", align_bytes=64)
        s_codes = pool.tile([P, E], U32, name="s_codes", align_bytes=64)
        s_scales = pool.tile([P, E], U8, name="s_scales", align_bytes=64)
        weight_row = pool.tile([P, PM, PACK], F32, name="weight_row", align_bytes=64)
        qa_blocks = pool.tile([P, PACK, ROWS], F32, name="qa_blocks", align_bytes=64)
        qa_turned = pool.tile([P, PACK, ROWS], F32, name="qa_turned", align_bytes=64)
        nc.vector.memset(qa_blocks[:], 0.0)
        for h in range(H):
            first = slice(ROWS * h, ROWS * h + 1)
            nc.vector.tensor_copy(out=qa_blocks[first], in_=qa_row[first, :].rearrange("o (p j) -> o j p", j=PACK))
        nc.vector.transpose(out=qa_turned[:].rearrange("p j c -> p (j c)"), in_=qa_blocks[:].rearrange("p j c -> p (j c)"))
        nc.vector.tensor_copy(out=weight_row[:], in_=qa_turned[:, :, 0].unsqueeze(1).to_broadcast([P, PM, PACK]))
        weight_bc = weight_row[:].rearrange("p m j -> p (m j)").unsqueeze(1).to_broadcast([P, R, PM * PACK])
        sums = {b: psum.tile([P, R, E], F32, name="sums%d_%d" % b) for b in blocks}

        def map_queries(half, piece):
            n0 = half * HN + piece * PIECE_W
            c, col = divmod(n0, LOAD_W)
            sq = pool.tile([P, R, PM, PACK], F32, name="sq%d_%d" % (half, piece), align_bytes=64)
            src = q_raw[c][:, :, col : col + PIECE_W].rearrange("p j (m r) -> p m j r", r=R)
            nc.scalar.activation(out=sq[:].rearrange("p r m j -> p m j r"), in_=src, func=ACT.Square)
            nc.vector.scalar_tensor_tensor(
                out=mapped[half][:, :, piece * PM : (piece + 1) * PM, :].rearrange("p r m j -> p r (m j)"),
                in0=sq[:].rearrange("p r m j -> p r (m j)"), scalar=0.125, in1=weight_bc,
                op0=ALU.add, op1=ALU.mult)

        def quantise_queries(half):
            nc.vector.quantize_mx(out=q_codes[half][:].bitcast(FP8X4), scales=q_scales[half][:],
                                  in_=mapped[half][:].rearrange("p r m j -> p (r m j)"))

        def multiply(half, heads):
            for r in range(R):
                cols = slice(r * P, (r + 1) * P)
                for h in heads:
                    rows = slice(ROWS * h, ROWS * (h + 1))
                    nc.tensor.matmul_mx(
                        out=sums[half, h][:, r, :], lhsT=q_codes[half][rows, cols].bitcast(FP8X4),
                        lhsT_scale=q_scales[half][rows, cols], rhs=s_codes[rows, :].bitcast(FP8X4),
                        rhs_scale=s_scales[rows, :], start=True, stop=True)

        def apply_gate(b, parts):
            part_w = R * E // parts
            for lo in range(0, R * E, part_w):
                cols = slice(lo, lo + part_w)
                fresh = slice(lo, min(lo + part_w, og_raw[b].shape[1]))
                nc.scalar.activation(out=gate[b][:, fresh], in_=og_raw[b][:, fresh], func=ACT.Sigmoid)
                res = pool.tile([P, part_w], F32, name="res%d_%d_%d" % (*b, lo), align_bytes=64)
                nc.vector.tensor_tensor(out=res[:], in0=sums[b][:].rearrange("p r e -> p (r e)")[:, cols],
                                        in1=gate[b][:, cols], op=ALU.mult)
                nc.sync.dma_start(out=block_rows(out, *b)[:, cols], in_=res[:])

        for piece in range(PIECES):
            map_queries(0, piece)
        nc.scalar.copy(out=s_bf[:], in_=s_raw[:].rearrange("p j e -> p e j"))
        nc.vector.quantize_mx(out=s_codes[:].bitcast(FP8X4), scales=s_scales[:],
                              in_=s_bf[:].rearrange("p e j -> p (e j)"))
        quantise_queries(0)
        multiply(0, range(H))
        for piece in range(PIECES):
            map_queries(1, piece)
        apply_gate((0, 0), 1)
        quantise_queries(1)
        multiply(1, range(H))
        for b in blocks[1:]:
            apply_gate(b, 1)
